import numpy as np
import ml_dtypes


def mxq(x, axis, fmt="e4m3"):
    dtype, down = {"e4m3": (ml_dtypes.float8_e4m3fn, 7), "e5m2": (ml_dtypes.float8_e5m2, 14)}[fmt]
    v = np.moveaxis(np.asarray(x, np.float32).astype(ml_dtypes.bfloat16).astype(np.float64), axis, -1)
    blocks = v.reshape(v.shape[:-1] + (-1, 32))
    amax = np.abs(blocks).max(-1, keepdims=True)
    byte = np.maximum(np.where(amax > 0, np.frexp(amax)[1] - 1 + 127, 0) - down, 1)
    scale = np.exp2(byte - 127.0)
    codes = (blocks / scale).astype(np.float32).astype(dtype).astype(np.float64)
    return np.moveaxis((codes * scale).reshape(v.shape), -1, axis)


WIDE = False


def mx_kscale(k):
    if not WIDE:
        return np.ones(k)
    levels = np.array([10, -10, 5, -5, 0])
    if k % 512:
        return np.exp2(np.random.permutation(np.resize(levels, k // 32))).repeat(32)
    a = np.empty((k // 512, 16))
    for p in range(k // 512):
        a[p, :8] = np.random.permutation(np.resize(levels, 8))
        for g in range(8):
            far = levels[np.abs(levels - a[p, g]) >= 10]
            a[p, g + 8] = far[np.random.randint(len(far))]
    return np.exp2(a.ravel()).repeat(32)


def f64(x):
    return np.asarray(x).astype(np.float64)


def striped(idx):
    return np.tile(idx.reshape(-1, 16).T, (8, 1)).astype(np.uint16)


def unstriped(offs):
    return offs[:16].T.reshape(-1).astype(np.int64)


def striped8(idx):
    return np.concatenate([x.reshape(-1, 16).T for x in idx]).astype(np.uint16)


def runs(offs, k):
    lists = np.stack([offs[16 * r : 16 * r + 16].T.reshape(-1) for r in range(8)]).astype(np.int64)
    return lists[np.arange(k) % 512 // 64]


def pack_weight(w):
    k, n = w.shape
    w = f64(np.asarray(w, np.float32).astype(ml_dtypes.bfloat16)).reshape(k // 32, 32, n)
    amax = np.abs(w).max(1)
    byte = np.clip(np.where(amax > 0, np.frexp(amax)[1] - 1 + 127 - 7, 1), 1, 254)
    scaled = (w * np.exp2(127.0 - byte)[:, None, :]).reshape(k, n).astype(np.float32)
    words = np.ascontiguousarray(scaled.reshape(k // 512, 128, 4, n).transpose(0, 1, 3, 2)).astype(ml_dtypes.float8_e4m3fn).view(np.uint8)
    return words, np.ascontiguousarray(byte.astype(np.uint8).reshape(k // 512, 16, n))


def unpack_weight(words, scales):
    g, p, n, _ = words.shape
    vals = np.ascontiguousarray(words).view(ml_dtypes.float8_e4m3fn).astype(np.float64) * np.repeat(np.exp2(scales.astype(np.float64) - 127.0), 8, axis=1)[..., None]
    return vals.transpose(0, 1, 3, 2).reshape(g * 512, n)


E2M1 = np.array([0.0, 0.5, 1.0, 1.5, 2.0, 3.0, 4.0, 6.0, -0.0, -0.5, -1.0, -1.5, -2.0, -3.0, -4.0, -6.0])


def pack_fp4(w):
    k, n = w.shape
    w = f64(np.asarray(w, np.float32).astype(ml_dtypes.bfloat16)).reshape(k // 32, 32, n)
    amax = np.abs(w).max(1)
    mant, ex = np.frexp(amax / 6.0)
    byte = np.clip(np.where(amax > 0, np.where(mant > 0.5, ex, ex - 1) + 127, 1), 1, 254)
    scaled = (w * np.exp2(127.0 - byte)[:, None, :]).reshape(k, n).astype(np.float32)
    c = np.ascontiguousarray(scaled.reshape(k // 512, 128, 4, n).transpose(0, 1, 3, 2)).astype(ml_dtypes.float4_e2m1fn).view(np.uint8) & 0xF
    words = (c[..., 0::2] | (c[..., 1::2] << 4)).reshape(k // 512, 128, 2 * n)
    return np.ascontiguousarray(words), np.ascontiguousarray(byte.astype(np.uint8).reshape(k // 512, 16, n))


def unpack_fp4(words, scales):
    g, _, n = scales.shape
    words = np.ascontiguousarray(words).reshape(g, 128, n, 2)
    nib = np.empty((g, 128, n, 4), np.uint8)
    nib[..., 0::2] = words & 0xF
    nib[..., 1::2] = words >> 4
    vals = E2M1[nib] * np.repeat(np.exp2(scales.astype(np.float64) - 127.0), 8, axis=1)[..., None]
    return vals.transpose(0, 1, 3, 2).reshape(g * 512, n)


def sigmoid(v):
    return 1.0 / (1.0 + np.exp(-np.maximum(v, -700.0)))

def planes(y):
    n, m = y.shape
    v = y.astype(np.float32).astype(ml_dtypes.bfloat16).astype(np.float64).reshape(n // 32, 32, m)
    top = np.abs(v).max(1)
    byte = np.clip(np.where(top > 0, np.frexp(top)[1] - 1 + 127 - 7, 1), 1, 254)
    codes = (v * np.exp2(127.0 - byte)[:, None, :]).reshape(n, m).astype(np.float32).astype(ml_dtypes.float8_e4m3fn).view(np.uint8)
    words = codes.reshape(n // 512, 128, 4, m).transpose(0, 1, 3, 2)
    return np.ascontiguousarray(words), np.ascontiguousarray(byte.astype(np.uint8).reshape(n // 512, 16, m))


K, T, S, N, H, W = 512, 2048, 512, 512, 512, 256


def setup_inputs():
    n = np.random.standard_normal
    s = mx_kscale(K)[:, None]
    u = mx_kscale(H)
    packed_xT = pack_weight(n((K, T)) * s)
    packed_w1 = pack_fp4(n((K, H)) / np.sqrt(K) / s)
    packed_w2 = pack_fp4(n((H, N)) / np.sqrt(2 * H) / u[:, None])
    packed_w3 = pack_fp4(n((H, N)) / np.sqrt(2 * H) / u[:, None])
    perm = np.stack([np.random.permutation(S) for _ in range(8)])
    return {
        "x_words": packed_xT[0],
        "x_scales": packed_xT[1],
        "w1_words": packed_w1[0],
        "w1_scales": packed_w1[1],
        "gn": (np.random.uniform(0.5, 1.5, (H, 1)) * u[:, None]).astype(np.float32),
        "gm": (np.random.uniform(0.5, 1.5, (H, 1)) * u[:, None]).astype(np.float32),
        "w2_words": packed_w2[0],
        "w2_scales": packed_w2[1],
        "w3_words": packed_w3[0],
        "w3_scales": packed_w3[1],
        "offs": striped(np.random.permutation(T)[:S]),
        "n1": striped8(np.stack([np.random.permutation(S) for _ in range(8)])),
        "n2": striped8(np.stack([np.random.permutation(S) for _ in range(8)])),
        "n3": striped8(np.stack([np.random.permutation(S) for _ in range(8)])),
        "n4": striped8(np.stack([np.random.permutation(S) for _ in range(8)])),
        "n5": striped8(perm[:, :W]),
        "n6": striped8(perm[:, W:]),
    }


def reference(x_words, x_scales, w1_words, w1_scales, gn, gm, w2_words, w2_scales, w3_words, w3_scales, offs, n1, n2, n3, n4, n5, n6):
    xq = unpack_weight(x_words, x_scales)[:, unstriped(offs)]
    y = unpack_fp4(w1_words, w1_scales).T @ xq
    sm = np.maximum(y, y[np.arange(H)[:, None], runs(n2, H)])
    ds = np.zeros((H, S))
    ds[np.arange(H)[:, None], runs(n1, H)] = sm
    z = f64(gn) * (ds * sigmoid(y))
    ex = np.exp(0.5 * y)
    z2 = f64(gm) * ((2.0 * ex) / (ex + ex[np.arange(H)[:, None], runs(n3, H)] + ex[np.arange(H)[:, None], runs(n4, H)]))
    h = unpack_fp4(w2_words, w2_scales).T @ mxq(z, 0, "e4m3") + unpack_fp4(w3_words, w3_scales).T @ mxq(z2, 0, "e4m3")
    pa = h[np.arange(N)[:, None], runs(n5, N)]
    pb = h[np.arange(N)[:, None], runs(n6, N)]
    rb = np.maximum(0.5 * pa, pb)
    ra = pb - pa
    ds2 = np.zeros((N, S))
    ds2[np.arange(N)[:, None], runs(n5, N)] = ra
    out = ds2.copy()
    out[np.arange(N)[:, None], runs(n6, N)] = rb
    return (out,) + planes(out)

@@ -1,0 +1,299 @@
+from contextlib import ExitStack
+
+import concourse.mybir as mybir
+from concourse.masks import make_identity
+
+F32 = mybir.dt.float32
+BF16 = mybir.dt.bfloat16
+I32 = mybir.dt.int32
+U32 = mybir.dt.uint32
+U16 = mybir.dt.uint16
+U8 = mybir.dt.uint8
+FP8X4 = mybir.dt.float8_e4m3fn_x4
+FP4X4 = mybir.dt.float4_e2m1fn_x4
+ALU = mybir.AluOpType
+ACT = mybir.ActivationFunctionType
+
+P = 128
+PACK = 4
+T = 2048
+S = 512
+HALF = 256
+FLOPS = 3 * 2 * 512 * 512 * 512
+
+
+def tile_picked_joinsendgsharelift_none_po_kernel(
+    tc, x_words, x_scales, w1_words, w1_scales, gn, gm, w2_words, w2_scales, w3_words, w3_scales,
+    offs, n1, n2, n3, n4, n5, n6, out_0, out_1, out_2,
+):
+    nc = tc.nc
+    with ExitStack() as ctx:
+        lists = ctx.enter_context(tc.tile_pool(name="lists", bufs=1))
+        sb = ctx.enter_context(tc.tile_pool(name="sb", bufs=1))
+        psum = ctx.enter_context(tc.psum_pool(name="psum", bufs=1))
+
+        def tile(name, shape, dtype):
+            return sb.tile(shape, dtype, name=name, align_bytes=64)
+
+        def load_list(name, src):
+            dst = lists.tile(list(src.shape), U16, name=name)
+            nc.sync.dma_start(dst[:], src)
+            return dst
+
+        def load_scale_rows(dst, src, queues):
+            for q in range(4):
+                queues[q].dma_start(dst[32 * q : 32 * q + 4, :].bitcast(I32), src[0, 4 * q : 4 * q + 4, :].bitcast(I32))
+
+        def half(lst, u):
+            return lst[:, 16 * u : 16 * u + 16]
+
+        xs_all = tile("xs_all", [P, T], U8)
+        nc.gpsimd.memset(xs_all[:].bitcast(I32), 0)
+        ws_raw = [tile("ws_raw%d" % i, [P, S], U8) for i in range(3)]
+        for raw in ws_raw:
+            nc.vector.memset(raw[:].bitcast(I32), 0)
+        ww_raw = [tile("ww_raw%d" % i, [P, 2 * S], U8) for i in range(3)]
+        offs_t = load_list("offs_t", offs)
+        load_scale_rows(xs_all, x_scales, (nc.sync, nc.sync, nc.scalar, nc.scalar))
+        nc.sync.dma_start(ww_raw[0][:].bitcast(I32), w1_words[0].bitcast(I32))
+        xw_all = tile("xw_all", [P, T], I32)
+        nc.sync.dma_start(xw_all[:], x_words[0].rearrange("p n t -> p (n t)").bitcast(I32))
+        load_scale_rows(ws_raw[0], w1_scales, (nc.sync,) * 4)
+        n2_t = load_list("n2_t", n2)
+        gn_t = tile("gn_t", [P, PACK], F32)
+        nc.sync.dma_start(gn_t[:], gn.rearrange("(p t) o -> p (t o)", t=PACK))
+        n1_t = load_list("n1_t", n1)
+        n3_t = load_list("n3_t", n3)
+        n4_t = load_list("n4_t", n4)
+        gm_t = tile("gm_t", [P, PACK], F32)
+        nc.sync.dma_start(gm_t[:], gm.rearrange("(p t) o -> p (t o)", t=PACK))
+        for i, (words, scales) in enumerate(((w2_words, w2_scales), (w3_words, w3_scales))):
+            nc.sync.dma_start(ww_raw[i + 1][:].bitcast(I32), words[0].bitcast(I32))
+            load_scale_rows(ws_raw[i + 1], scales, (nc.sync,) * 4)
+        n5_t = load_list("n5_t", n5)
+        n6_t = load_list("n6_t", n6)
+
+        ident = tile("ident", [P, P], F32)
+        make_identity(nc, ident[:])
+
+        ww = [tile("ww%d" % i, [P, 2 * S], U8) for i in range(3)]
+        ws = [tile("ws%d" % i, [P, S], U8) for i in range(3)]
+
+        def deal(i):
+            if i == 0:
+                nc.scalar.copy(
+                    ww[i][:].bitcast(U16).rearrange("p (t m) -> p t m", t=PACK),
+                    ww_raw[i][:].bitcast(U16).rearrange("p (m t) -> p t m", t=PACK),
+                )
+            else:
+                nc.gpsimd.tensor_copy(
+                    ww[i][:].rearrange("p (t m b) -> p t m b", t=PACK, b=2),
+                    ww_raw[i][:].rearrange("p (m t b) -> p t m b", t=PACK, b=2),
+                )
+            nc.gpsimd.tensor_copy(
+                ws[i][:].rearrange("p (t m) -> p t m", t=PACK),
+                ws_raw[i][:].rearrange("p (m t) -> p t m", t=PACK),
+            )
+
+        def product(dst, i, t, codes, scales, cols, start, stop):
+            nc.tensor.matmul_mx(
+                out=dst,
+                lhsT=ww[i][:, 2 * P * t : 2 * P * (t + 1)].bitcast(FP4X4),
+                lhsT_scale=ws[i][:, P * t : P * (t + 1)],
+                rhs=codes[:, cols].bitcast(FP8X4),
+                rhs_scale=scales[:, cols],
+                start=start,
+                stop=stop,
+            )
+
+        xs = tile("xs", [P, S], U8)
+        xw = tile("xw", [P, S], U32)
+        nc.vector.tensor_copy(xs[:], xs_all[:].indirect(offs_t[:]))
+        deal(0)
+        halves = [slice(0, HALF), slice(HALF, S)]
+        for u in range(2):
+            nc.vector.tensor_copy(xw[:, halves[u]], xw_all[:].bitcast(U32).indirect(half(offs_t, u)))
+
+        y_bank = [psum.tile([P, S], F32, name="y_bank%d" % t, tag="a%d" % t) for t in range(PACK)]
+        for t in range(PACK):
+            for u in range(2):
+                product(y_bank[t][:, halves[u]], 0, t, xw, xs, halves[u], True, True)
+
+        gain = tile("gain", [P, PACK, S], F32)
+        nc.gpsimd.tensor_scalar(
+            gain[:], gn_t[:].unsqueeze(2).to_broadcast([P, PACK, S]), 0.5, 0.0, ALU.mult, ALU.add
+        )
+        gm2 = tile("gm2", [P, PACK], F32)
+        nc.gpsimd.tensor_scalar(gm2[:], gm_t[:], 2.0, 0.0, ALU.mult, ALU.add)
+
+        def gather(engine, dst, window, offsets):
+            if engine is nc.vector:
+                nc.vector.tensor_copy(dst, window[:].indirect(offsets))
+            else:
+                nc.scalar.activation(dst, window[:].indirect(offsets), ACT.Copy)
+
+        def planes(name):
+            return [tile("%s%d" % (name, t), [P, S], F32) for t in range(PACK)]
+
+        y, y2, sm, ex, ex3, ex4, th = (planes(n) for n in ("y", "y2", "sm", "ex", "ex3", "ex4", "th"))
+        ds = [tile("ds%d" % t, [P, 2 * S], F32) for t in range(PACK)]
+        den_bank = [psum.tile([P, PACK, P], F32, name="den_bank%d" % j, tag="b%d" % j) for j in range(PACK)]
+
+        def fetch_y(t, engine):
+            if engine is nc.vector:
+                nc.vector.tensor_copy(y[t][:], y_bank[t][:])
+            else:
+                nc.scalar.copy(y[t][:], y_bank[t][:])
+            for u in range(2):
+                gather(engine, y2[t][:, halves[u]], y[t], half(n2_t, u))
+
+        def send(t):
+            nc.vector.tensor_tensor(sm[t][:], y[t][:], y2[t][:], ALU.max)
+            nc.vector.tensor_tensor(ds[t][:].indirect(n1_t[:]), sm[t][:], gain[:, t, :], ALU.mult)
+
+        def funcs(t):
+            nc.scalar.activation(ex[t][:], y_bank[t][:], ACT.Exp, scale=0.5)
+
+        def tanh(t):
+            nc.scalar.activation(th[t][:], y_bank[t][:], ACT.Tanh, scale=0.5)
+
+        def fetch_ex(t, e3, e4):
+            for u in range(2):
+                gather(e3, ex3[t][:, halves[u]], ex[t], half(n3_t, u))
+            for u in range(2):
+                gather(e4, ex4[t][:, halves[u]], ex[t], half(n4_t, u))
+            for j in range(PACK):
+                for k, src in enumerate((ex[t], ex3[t], ex4[t])):
+                    nc.tensor.matmul(
+                        den_bank[j][:, t, :], src[:, P * j : P * (j + 1)], ident[:],
+                        start=(k == 0), stop=(k == 2), is_transpose=True,
+                    )
+
+        V, A = nc.vector, nc.scalar
+        deal(1)
+        deal(2)
+        zp = tile("zp", [P, PACK, S], BF16)
+        z2p = tile("z2p", [P, PACK, S], BF16)
+
+        def make_z(t):
+            nc.vector.scalar_tensor_tensor(zp[:, t, :], th[t][:], 1.0, ds[t][:, :S], ALU.add, ALU.mult)
+
+        def quantised(name):
+            return (tile(name + "_woven", [P, S * PACK], BF16), tile(name + "_codes", [P, S], U32),
+                    tile(name + "_scales", [P, S], U8))
+
+        def weave(copy, dst, src, u):
+            copy(
+                dst[0][:, PACK * HALF * u : PACK * HALF * (u + 1)].rearrange("p (c i t) -> p c t i", i=4, t=PACK),
+                src[:, :, halves[u]].rearrange("p t (c i) -> p c t i", i=4),
+            )
+
+        def quantise(dst, u):
+            nc.vector.quantize_mx(
+                out=dst[1][:, halves[u]].bitcast(FP8X4),
+                scales=dst[2][:, halves[u]],
+                in_=dst[0][:, PACK * HALF * u : PACK * HALF * (u + 1)],
+            )
+
+        fetch_y(0, V)
+        funcs(0)
+        fetch_y(1, A)
+        send(0)
+        funcs(1)
+        funcs(2)
+        funcs(3)
+        fetch_ex(0, A, V)
+        send(1)
+        fetch_y(2, A)
+        tanh(0)
+        fetch_ex(1, A, V)
+        send(2)
+        fetch_y(3, A)
+        tanh(1)
+        fetch_ex(2, A, A)
+        send(3)
+        fetch_ex(3, A, A)
+        for t in range(2, PACK):
+            tanh(t)
+        for t in range(PACK):
+            make_z(t)
+        zq, z2q = quantised("z"), quantised("z2")
+
+        root = tile("root", [P, PACK, S], F32)
+        rden = tile("rden", [P, PACK, S], F32)
+        r_bank = [psum.tile([P, 2, HALF], F32, name="r_bank%d" % b, tag="a%d" % b) for b in range(PACK)]
+        for u in range(2):
+            for j in (2 * u, 2 * u + 1):
+                nc.scalar.activation(root[:, j, :], den_bank[j][:].rearrange("p t n -> p (t n)"), ACT.Abs_reciprocal_sqrt)
+            for j in (2 * u, 2 * u + 1):
+                nc.scalar.activation(rden[:, j, :], root[:, j, :], ACT.Square)
+            for t in range(PACK):
+                for jj in range(2):
+                    nc.tensor.transpose(
+                        r_bank[2 * u + t // 2][:, t % 2, P * jj : P * (jj + 1)],
+                        rden[:, 2 * u + jj, P * t : P * (t + 1)], ident[:],
+                    )
+        for u in range(2):
+            weave(nc.scalar.copy, zq, zp, u)
+        h_bank = [[None] * PACK, [None] * PACK]
+        h = planes("h")
+        for u in range(2):
+            for t in range(PACK):
+                nc.vector.scalar_tensor_tensor(
+                    z2p[:, t, halves[u]], ex[t][:, halves[u]], gm2[:, t : t + 1], r_bank[2 * u + t // 2][:, t % 2, :],
+                    ALU.mult, ALU.mult,
+                )
+            quantise(zq, u)
+            weave(nc.vector.tensor_copy, z2q, z2p, u)
+            quantise(z2q, u)
+            first, last = ((2, z2q), (1, zq)) if u == 0 else ((1, zq), (2, z2q))
+            for t in range(PACK):
+                h_bank[u][t] = psum.tile([P, HALF], F32, name="h_bank%d%d" % (u, t), tag="ba"[u] + str(t))
+                product(h_bank[u][t][:], first[0], t, first[1][1], first[1][2], halves[u], True, False)
+            for t in range(PACK):
+                product(h_bank[u][t][:], last[0], t, last[1][1], last[1][2], halves[u], False, True)
+        for t in range(PACK):
+            nc.scalar.copy(h[t][:, halves[0]], h_bank[0][t][:])
+
+        res = planes("res")
+        npa = tile("npa", [P, PACK, HALF], F32)
+        pb = tile("pb", [P, PACK, HALF], F32)
+        rb = tile("rb", [P, PACK, HALF], F32)
+        out_rows = out_0.rearrange("(p t) n -> p t n", t=PACK)
+        o_woven = tile("o_woven", [P, S, PACK], BF16)
+        o_codes = tile("o_codes", [P, S], I32)
+        o_scales = tile("o_scales", [P, S], U8)
+        for t in range(PACK):
+            nc.scalar.copy(h[t][:, halves[1]], h_bank[1][t][:])
+            nc.scalar.activation(npa[:, t, :], h[t][:].indirect(n5_t[:]), ACT.Copy, scale=-1.0)
+            gather(V if t == 0 else A, pb[:, t, :], h[t], n6_t[:])
+
+        def put_a(t):
+            nc.vector.scalar_tensor_tensor(rb[:, t, :], npa[:, t, :], -0.5, pb[:, t, :], ALU.mult, ALU.max)
+            nc.vector.tensor_tensor(res[t][:].indirect(n5_t[:]), pb[:, t, :], npa[:, t, :], ALU.add)
+
+        def put_b(t):
+            nc.vector.tensor_copy(res[t][:].indirect(n6_t[:]), rb[:, t, :])
+            nc.sync.dma_start(out_rows[:, t, :], res[t][:])
+            nc.scalar.copy(o_woven[:, halves[0], t], res[t][:, halves[0]])
+            if t < 2:
+                nc.scalar.copy(o_woven[:, halves[1], t], res[t][:, halves[1]])
+            else:
+                nc.vector.tensor_copy(o_woven[:, halves[1], t], res[t][:, halves[1]])
+
+        put_a(0)
+        for t in range(1, PACK):
+            put_a(t)
+            put_b(t - 1)
+        put_b(PACK - 1)
+        words_out = out_1[0].rearrange("p n t -> p (n t)").bitcast(I32)
+        for u in (1, 0):
+            nc.vector.quantize_mx(
+                out=o_codes[:, halves[u]].bitcast(FP8X4),
+                scales=o_scales[:, halves[u]],
+                in_=o_woven[:, halves[u], :].rearrange("p n t -> p (n t)"),
+            )
+            nc.sync.dma_start(words_out[:, halves[u]], o_codes[:, halves[u]])
+        for q in range(4):
+            queue = nc.scalar if q % 2 else nc.sync
+            queue.dma_start(out_2[0, 4 * q : 4 * q + 4, :].bitcast(I32), o_scales[32 * q : 32 * q + 4, :].bitcast(I32))

@@ -49,48 +49,42 @@ def tile_picked_joinsendgsharelift_none_po_kernel(
 
         xs_all = tile("xs_all", [P, T], U8)
         nc.gpsimd.memset(xs_all[:].bitcast(I32), 0)
+        ident = tile("ident", [P, P], F32)
+        make_identity(nc, ident[:])
         ws_raw = [tile("ws_raw%d" % i, [P, S], U8) for i in range(3)]
         for raw in ws_raw:
-            nc.vector.memset(raw[:].bitcast(I32), 0)
+            nc.gpsimd.memset(raw[:].bitcast(I32), 0)
         ww_raw = [tile("ww_raw%d" % i, [P, 2 * S], U8) for i in range(3)]
         offs_t = load_list("offs_t", offs)
         load_scale_rows(xs_all, x_scales, (nc.sync, nc.sync, nc.scalar, nc.scalar))
         nc.sync.dma_start(ww_raw[0][:].bitcast(I32), w1_words[0].bitcast(I32))
+        gn_t = tile("gn_t", [P, PACK], F32)
+        nc.scalar.dma_start(gn_t[:], gn.rearrange("(p t) o -> p (t o)", t=PACK))
         xw_all = tile("xw_all", [P, T], I32)
         nc.sync.dma_start(xw_all[:], x_words[0].rearrange("p n t -> p (n t)").bitcast(I32))
         load_scale_rows(ws_raw[0], w1_scales, (nc.sync,) * 4)
+        nc.sync.dma_start(ww_raw[1][:].bitcast(I32), w2_words[0].bitcast(I32))
+        nc.sync.dma_start(ww_raw[2][:].bitcast(I32), w3_words[0].bitcast(I32))
         n2_t = load_list("n2_t", n2)
-        gn_t = tile("gn_t", [P, PACK], F32)
-        nc.sync.dma_start(gn_t[:], gn.rearrange("(p t) o -> p (t o)", t=PACK))
         n1_t = load_list("n1_t", n1)
-        n3_t = load_list("n3_t", n3)
         n4_t = load_list("n4_t", n4)
+        n3_t = load_list("n3_t", n3)
+        load_scale_rows(ws_raw[1], w2_scales, (nc.sync,) * 4)
+        load_scale_rows(ws_raw[2], w3_scales, (nc.sync,) * 4)
         gm_t = tile("gm_t", [P, PACK], F32)
         nc.sync.dma_start(gm_t[:], gm.rearrange("(p t) o -> p (t o)", t=PACK))
-        for i, (words, scales) in enumerate(((w2_words, w2_scales), (w3_words, w3_scales))):
-            nc.sync.dma_start(ww_raw[i + 1][:].bitcast(I32), words[0].bitcast(I32))
-            load_scale_rows(ws_raw[i + 1], scales, (nc.sync,) * 4)
         n5_t = load_list("n5_t", n5)
         n6_t = load_list("n6_t", n6)
-
-        ident = tile("ident", [P, P], F32)
-        make_identity(nc, ident[:])
 
         ww = [tile("ww%d" % i, [P, 2 * S], U8) for i in range(3)]
         ws = [tile("ws%d" % i, [P, S], U8) for i in range(3)]
 
         def deal(i):
-            if i == 0:
-                nc.scalar.copy(
-                    ww[i][:].bitcast(U16).rearrange("p (t m) -> p t m", t=PACK),
-                    ww_raw[i][:].bitcast(U16).rearrange("p (m t) -> p t m", t=PACK),
-                )
-            else:
-                nc.gpsimd.tensor_copy(
-                    ww[i][:].rearrange("p (t m b) -> p t m b", t=PACK, b=2),
-                    ww_raw[i][:].rearrange("p (m t b) -> p t m b", t=PACK, b=2),
-                )
-            nc.gpsimd.tensor_copy(
+            nc.scalar.copy(
+                ww[i][:].bitcast(U16).rearrange("p (t m) -> p t m", t=PACK),
+                ww_raw[i][:].bitcast(U16).rearrange("p (m t) -> p t m", t=PACK),
+            )
+            nc.vector.tensor_copy(
                 ws[i][:].rearrange("p (t m) -> p t m", t=PACK),
                 ws_raw[i][:].rearrange("p (m t) -> p t m", t=PACK),
             )
@@ -115,16 +109,15 @@ def tile_picked_joinsendgsharelift_none_po_kernel(
             nc.vector.tensor_copy(xw[:, halves[u]], xw_all[:].bitcast(U32).indirect(half(offs_t, u)))
 
         y_bank = [psum.tile([P, S], F32, name="y_bank%d" % t, tag="a%d" % t) for t in range(PACK)]
-        for t in range(PACK):
+        y_first = psum.tile([P, HALF], F32, name="y_first", tag="b3")
+        product(y_first[:], 0, 0, xw, xs, halves[0], True, True)
+        product(y_bank[0][:, halves[1]], 0, 0, xw, xs, halves[1], True, True)
+        for t in range(1, PACK):
             for u in range(2):
                 product(y_bank[t][:, halves[u]], 0, t, xw, xs, halves[u], True, True)
 
         gain = tile("gain", [P, PACK, S], F32)
-        nc.gpsimd.tensor_scalar(
-            gain[:], gn_t[:].unsqueeze(2).to_broadcast([P, PACK, S]), 0.5, 0.0, ALU.mult, ALU.add
-        )
-        gm2 = tile("gm2", [P, PACK], F32)
-        nc.gpsimd.tensor_scalar(gm2[:], gm_t[:], 2.0, 0.0, ALU.mult, ALU.add)
+        nc.scalar.activation(gain[:], gn_t[:].unsqueeze(2).to_broadcast([P, PACK, S]), ACT.Copy, scale=0.5)
 
         def gather(engine, dst, window, offsets):
             if engine is nc.vector:
@@ -140,8 +133,9 @@ def tile_picked_joinsendgsharelift_none_po_kernel(
         den_bank = [psum.tile([P, PACK, P], F32, name="den_bank%d" % j, tag="b%d" % j) for j in range(PACK)]
 
         def fetch_y(t, engine):
-            if engine is nc.vector:
-                nc.vector.tensor_copy(y[t][:], y_bank[t][:])
+            if t == 0:
+                nc.scalar.copy(y[t][:, halves[0]], y_first[:])
+                nc.vector.tensor_copy(y[t][:, halves[1]], y_bank[t][:, halves[1]])
             else:
                 nc.scalar.copy(y[t][:], y_bank[t][:])
             for u in range(2):
@@ -152,10 +146,10 @@ def tile_picked_joinsendgsharelift_none_po_kernel(
             nc.vector.tensor_tensor(ds[t][:].indirect(n1_t[:]), sm[t][:], gain[:, t, :], ALU.mult)
 
         def funcs(t):
-            nc.scalar.activation(ex[t][:], y_bank[t][:], ACT.Exp, scale=0.5)
+            nc.scalar.activation(ex[t][:], (y_bank[t] if t else y[t])[:], ACT.Exp, scale=0.5)
 
         def tanh(t):
-            nc.scalar.activation(th[t][:], y_bank[t][:], ACT.Tanh, scale=0.5)
+            nc.scalar.activation(th[t][:], (y_bank[t] if t else y[t])[:], ACT.Tanh, scale=0.5)
 
         def fetch_ex(t, e3, e4):
             for u in range(2):
@@ -224,7 +218,7 @@ def tile_picked_joinsendgsharelift_none_po_kernel(
         r_bank = [psum.tile([P, 2, HALF], F32, name="r_bank%d" % b, tag="a%d" % b) for b in range(PACK)]
         for u in range(2):
             for j in (2 * u, 2 * u + 1):
-                nc.scalar.activation(root[:, j, :], den_bank[j][:].rearrange("p t n -> p (t n)"), ACT.Abs_reciprocal_sqrt)
+                nc.scalar.activation(root[:, j, :], den_bank[j][:].rearrange("p t n -> p (t n)"), ACT.Abs_reciprocal_sqrt, scale=0.5)
             for j in (2 * u, 2 * u + 1):
                 nc.scalar.activation(rden[:, j, :], root[:, j, :], ACT.Square)
             for t in range(PACK):
@@ -240,18 +234,21 @@ def tile_picked_joinsendgsharelift_none_po_kernel(
         for u in range(2):
             for t in range(PACK):
                 nc.vector.scalar_tensor_tensor(
-                    z2p[:, t, halves[u]], ex[t][:, halves[u]], gm2[:, t : t + 1], r_bank[2 * u + t // 2][:, t % 2, :],
+                    z2p[:, t, halves[u]], ex[t][:, halves[u]], gm_t[:, t : t + 1], r_bank[2 * u + t // 2][:, t % 2, :],
                     ALU.mult, ALU.mult,
                 )
             quantise(zq, u)
             weave(nc.vector.tensor_copy, z2q, z2p, u)
             quantise(z2q, u)
-            first, last = ((2, z2q), (1, zq)) if u == 0 else ((1, zq), (2, z2q))
             for t in range(PACK):
                 h_bank[u][t] = psum.tile([P, HALF], F32, name="h_bank%d%d" % (u, t), tag="ba"[u] + str(t))
-                product(h_bank[u][t][:], first[0], t, first[1][1], first[1][2], halves[u], True, False)
-            for t in range(PACK):
-                product(h_bank[u][t][:], last[0], t, last[1][1], last[1][2], halves[u], False, True)
+            if u == 1:
+                product(h_bank[u][0][:], 1, 0, zq[1], zq[2], halves[u], True, False)
+                product(h_bank[u][0][:], 2, 0, z2q[1], z2q[2], halves[u], False, True)
+            for t in range(u, PACK):
+                product(h_bank[u][t][:], 2, t, z2q[1], z2q[2], halves[u], True, False)
+            for t in range(u, PACK):
+                product(h_bank[u][t][:], 1, t, zq[1], zq[2], halves[u], False, True)
         for t in range(PACK):
             nc.scalar.copy(h[t][:, halves[0]], h_bank[0][t][:])
 
@@ -269,7 +266,6 @@ def tile_picked_joinsendgsharelift_none_po_kernel(
             gather(V if t == 0 else A, pb[:, t, :], h[t], n6_t[:])
 
         def put_a(t):
-            nc.vector.scalar_tensor_tensor(rb[:, t, :], npa[:, t, :], -0.5, pb[:, t, :], ALU.mult, ALU.max)
             nc.vector.tensor_tensor(res[t][:].indirect(n5_t[:]), pb[:, t, :], npa[:, t, :], ALU.add)
 
         def put_b(t):
@@ -281,11 +277,14 @@ def tile_picked_joinsendgsharelift_none_po_kernel(
             else:
                 nc.vector.tensor_copy(o_woven[:, halves[1], t], res[t][:, halves[1]])
 
-        put_a(0)
-        for t in range(1, PACK):
+        for t in (0, 2):
             put_a(t)
-            put_b(t - 1)
-        put_b(PACK - 1)
+            nc.vector.scalar_tensor_tensor(
+                rb[:, t : t + 2, :], npa[:, t : t + 2, :], -0.5, pb[:, t : t + 2, :], ALU.mult, ALU.max
+            )
+            put_a(t + 1)
+            put_b(t)
+            put_b(t + 1)
         words_out = out_1[0].rearrange("p n t -> p (n t)").bitcast(I32)
         for u in (1, 0):
             nc.vector.quantize_mx(

@@ -48,27 +48,27 @@ def tile_picked_joinsendgsharelift_none_po_kernel(
             return lst[:, 16 * u : 16 * u + 16]
 
         xs_all = tile("xs_all", [P, T], U8)
-        nc.gpsimd.memset(xs_all[:].bitcast(I32), 0)
-        ident = tile("ident", [P, P], F32)
-        make_identity(nc, ident[:])
+        nc.vector.memset(xs_all[:].bitcast(I32), 0)
         ws_raw = [tile("ws_raw%d" % i, [P, S], U8) for i in range(3)]
         for raw in ws_raw:
             nc.gpsimd.memset(raw[:].bitcast(I32), 0)
+        ident = tile("ident", [P, P], F32)
+        make_identity(nc, ident[:])
         ww_raw = [tile("ww_raw%d" % i, [P, 2 * S], U8) for i in range(3)]
         offs_t = load_list("offs_t", offs)
         load_scale_rows(xs_all, x_scales, (nc.sync, nc.sync, nc.scalar, nc.scalar))
         nc.sync.dma_start(ww_raw[0][:].bitcast(I32), w1_words[0].bitcast(I32))
-        gn_t = tile("gn_t", [P, PACK], F32)
-        nc.scalar.dma_start(gn_t[:], gn.rearrange("(p t) o -> p (t o)", t=PACK))
         xw_all = tile("xw_all", [P, T], I32)
         nc.sync.dma_start(xw_all[:], x_words[0].rearrange("p n t -> p (n t)").bitcast(I32))
         load_scale_rows(ws_raw[0], w1_scales, (nc.sync,) * 4)
-        nc.sync.dma_start(ww_raw[1][:].bitcast(I32), w2_words[0].bitcast(I32))
-        nc.sync.dma_start(ww_raw[2][:].bitcast(I32), w3_words[0].bitcast(I32))
         n2_t = load_list("n2_t", n2)
         n1_t = load_list("n1_t", n1)
         n4_t = load_list("n4_t", n4)
         n3_t = load_list("n3_t", n3)
+        gn_t = tile("gn_t", [P, PACK], F32)
+        nc.sync.dma_start(gn_t[:], gn.rearrange("(p t) o -> p (t o)", t=PACK))
+        nc.sync.dma_start(ww_raw[1][:].bitcast(I32), w2_words[0].bitcast(I32))
+        nc.sync.dma_start(ww_raw[2][:].bitcast(I32), w3_words[0].bitcast(I32))
         load_scale_rows(ws_raw[1], w2_scales, (nc.sync,) * 4)
         load_scale_rows(ws_raw[2], w3_scales, (nc.sync,) * 4)
         gm_t = tile("gm_t", [P, PACK], F32)
@@ -80,11 +80,17 @@ def tile_picked_joinsendgsharelift_none_po_kernel(
         ws = [tile("ws%d" % i, [P, S], U8) for i in range(3)]
 
         def deal(i):
-            nc.scalar.copy(
-                ww[i][:].bitcast(U16).rearrange("p (t m) -> p t m", t=PACK),
-                ww_raw[i][:].bitcast(U16).rearrange("p (m t) -> p t m", t=PACK),
-            )
-            nc.vector.tensor_copy(
+            if i == 0:
+                nc.scalar.copy(
+                    ww[i][:].bitcast(U16).rearrange("p (t m) -> p t m", t=PACK),
+                    ww_raw[i][:].bitcast(U16).rearrange("p (m t) -> p t m", t=PACK),
+                )
+            else:
+                nc.gpsimd.tensor_copy(
+                    ww[i][:].rearrange("p (t m b) -> p t m b", t=PACK, b=2),
+                    ww_raw[i][:].rearrange("p (m t b) -> p t m b", t=PACK, b=2),
+                )
+            nc.gpsimd.tensor_copy(
                 ws[i][:].rearrange("p (t m) -> p t m", t=PACK),
                 ws_raw[i][:].rearrange("p (m t) -> p t m", t=PACK),
             )
@@ -116,8 +122,8 @@ def tile_picked_joinsendgsharelift_none_po_kernel(
             for u in range(2):
                 product(y_bank[t][:, halves[u]], 0, t, xw, xs, halves[u], True, True)
 
-        gain = tile("gain", [P, PACK, S], F32)
-        nc.scalar.activation(gain[:], gn_t[:].unsqueeze(2).to_broadcast([P, PACK, S]), ACT.Copy, scale=0.5)
+        gain = tile("gain", [P, PACK], F32)
+        nc.gpsimd.tensor_scalar(gain[:], gn_t[:], 0.5, 0.0, ALU.mult, ALU.add)
 
         def gather(engine, dst, window, offsets):
             if engine is nc.vector:
@@ -129,27 +135,31 @@ def tile_picked_joinsendgsharelift_none_po_kernel(
             return [tile("%s%d" % (name, t), [P, S], F32) for t in range(PACK)]
 
         y, y2, sm, ex, ex3, ex4, th = (planes(n) for n in ("y", "y2", "sm", "ex", "ex3", "ex4", "th"))
+        gate = planes("gate")
         ds = [tile("ds%d" % t, [P, 2 * S], F32) for t in range(PACK)]
         den_bank = [psum.tile([P, PACK, P], F32, name="den_bank%d" % j, tag="b%d" % j) for j in range(PACK)]
 
-        def fetch_y(t, engine):
+        def take_y(t):
             if t == 0:
                 nc.scalar.copy(y[t][:, halves[0]], y_first[:])
                 nc.vector.tensor_copy(y[t][:, halves[1]], y_bank[t][:, halves[1]])
             else:
                 nc.scalar.copy(y[t][:], y_bank[t][:])
+
+        def fetch_y(t, engine):
             for u in range(2):
                 gather(engine, y2[t][:, halves[u]], y[t], half(n2_t, u))
 
         def send(t):
-            nc.vector.tensor_tensor(sm[t][:], y[t][:], y2[t][:], ALU.max)
-            nc.vector.tensor_tensor(ds[t][:].indirect(n1_t[:]), sm[t][:], gain[:, t, :], ALU.mult)
+            nc.vector.tensor_tensor(sm[t][:], y2[t][:], (y_bank[t] if t else y[t])[:], ALU.max)
+            nc.vector.tensor_copy(ds[t][:].indirect(n1_t[:]), sm[t][:])
 
-        def funcs(t):
-            nc.scalar.activation(ex[t][:], (y_bank[t] if t else y[t])[:], ACT.Exp, scale=0.5)
+        def funcs(t, cols=slice(0, S)):
+            nc.scalar.activation(ex[t][:, cols], (y_bank[t] if t else y[t])[:, cols], ACT.Exp, scale=0.5)
 
         def tanh(t):
-            nc.scalar.activation(th[t][:], (y_bank[t] if t else y[t])[:], ACT.Tanh, scale=0.5)
+            nc.scalar.activation(th[t][:], y[t][:], ACT.Tanh, scale=0.5)
+            nc.gpsimd.tensor_scalar(gate[t][:], th[t][:], gain[:, t : t + 1], gain[:, t : t + 1], ALU.mult, ALU.add)
 
         def fetch_ex(t, e3, e4):
             for u in range(2):
@@ -170,7 +180,8 @@ def tile_picked_joinsendgsharelift_none_po_kernel(
         z2p = tile("z2p", [P, PACK, S], BF16)
 
         def make_z(t):
-            nc.vector.scalar_tensor_tensor(zp[:, t, :], th[t][:], 1.0, ds[t][:, :S], ALU.add, ALU.mult)
+            for cols in halves if t == PACK - 1 else [slice(0, S)]:
+                nc.gpsimd.tensor_tensor(zp[:, t, cols], gate[t][:, cols], ds[t][:, cols], ALU.mult)
 
         def quantised(name):
             return (tile(name + "_woven", [P, S * PACK], BF16), tile(name + "_codes", [P, S], U32),
@@ -189,39 +200,49 @@ def tile_picked_joinsendgsharelift_none_po_kernel(
                 in_=dst[0][:, PACK * HALF * u : PACK * HALF * (u + 1)],
             )
 
+        take_y(0)
         fetch_y(0, V)
         funcs(0)
-        fetch_y(1, A)
+        take_y(1)
+        fetch_ex(0, A, V)
         send(0)
         funcs(1)
-        funcs(2)
-        funcs(3)
-        fetch_ex(0, A, V)
+        funcs(2, halves[0])
+        fetch_y(1, A)
+        funcs(2, halves[1])
+        take_y(2)
+        fetch_ex(2, A, V)
         send(1)
-        fetch_y(2, A)
         tanh(0)
-        fetch_ex(1, A, V)
+        make_z(0)
+        funcs(3, halves[0])
+        fetch_y(2, A)
+        funcs(3, halves[1])
+        take_y(3)
+        fetch_ex(3, A, V)
         send(2)
-        fetch_y(3, A)
         tanh(1)
-        fetch_ex(2, A, A)
+        make_z(1)
+        fetch_y(3, A)
+        fetch_ex(1, A, A)
         send(3)
-        fetch_ex(3, A, A)
-        for t in range(2, PACK):
-            tanh(t)
-        for t in range(PACK):
-            make_z(t)
+        tanh(2)
+        make_z(2)
+        tanh(3)
+        make_z(3)
         zq, z2q = quantised("z"), quantised("z2")
 
         root = tile("root", [P, PACK, S], F32)
         rden = tile("rden", [P, PACK, S], F32)
         r_bank = [psum.tile([P, 2, HALF], F32, name="r_bank%d" % b, tag="a%d" % b) for b in range(PACK)]
         for u in range(2):
-            for j in (2 * u, 2 * u + 1):
-                nc.scalar.activation(root[:, j, :], den_bank[j][:].rearrange("p t n -> p (t n)"), ACT.Abs_reciprocal_sqrt, scale=0.5)
-            for j in (2 * u, 2 * u + 1):
-                nc.scalar.activation(rden[:, j, :], root[:, j, :], ACT.Square)
+            for j, cols in ((2 * u, slice(0, S)), (2 * u + 1, halves[0]), (2 * u + 1, halves[1])):
+                den = den_bank[j][:].rearrange("p t n -> p (t n)")
+                nc.scalar.activation(root[:, j, cols], den[:, cols], ACT.Abs_reciprocal_sqrt, scale=0.5)
             for t in range(PACK):
+                if t % 2 == 0:
+                    blocks, cols = slice(2 * u, 2 * u + 2), slice(P * t, P * (t + 2))
+                    nc.scalar.activation(rden[:, blocks, cols], root[:, blocks, cols], ACT.Square)
                 for jj in range(2):
                     nc.tensor.transpose(
                         r_bank[2 * u + t // 2][:, t % 2, P * jj : P * (jj + 1)],

from contextlib import ExitStack

import concourse.mybir as mybir
from concourse.masks import make_identity

F32 = mybir.dt.float32
BF16 = mybir.dt.bfloat16
I32 = mybir.dt.int32
U32 = mybir.dt.uint32
U16 = mybir.dt.uint16
U8 = mybir.dt.uint8
FP8X4 = mybir.dt.float8_e4m3fn_x4
FP4X4 = mybir.dt.float4_e2m1fn_x4
ALU = mybir.AluOpType
ACT = mybir.ActivationFunctionType

P = 128
PACK = 4
T = 2048
S = 512
HALF = 256
FLOPS = 3 * 2 * 512 * 512 * 512


def tile_picked_joinsendgsharelift_none_po_kernel(
    tc, x_words, x_scales, w1_words, w1_scales, gn, gm, w2_words, w2_scales, w3_words, w3_scales,
    offs, n1, n2, n3, n4, n5, n6, out_0, out_1, out_2,
):
    nc = tc.nc
    with ExitStack() as ctx:
        lists = ctx.enter_context(tc.tile_pool(name="lists", bufs=1))
        sb = ctx.enter_context(tc.tile_pool(name="sb", bufs=1))
        psum = ctx.enter_context(tc.psum_pool(name="psum", bufs=1))

        def tile(name, shape, dtype):
            return sb.tile(shape, dtype, name=name, align_bytes=64)

        def load_list(name, src):
            dst = lists.tile(list(src.shape), U16, name=name)
            nc.sync.dma_start(dst[:], src)
            return dst

        def load_scale_rows(dst, src, queues):
            for q in range(4):
                queues[q].dma_start(dst[32 * q : 32 * q + 4, :].bitcast(I32), src[0, 4 * q : 4 * q + 4, :].bitcast(I32))

        def half(lst, u):
            return lst[:, 16 * u : 16 * u + 16]

        xs_all = tile("xs_all", [P, T], U8)
        nc.vector.memset(xs_all[:].bitcast(I32), 0)
        ws_raw = [tile("ws_raw%d" % i, [P, S], U8) for i in range(3)]
        for raw in ws_raw:
            nc.gpsimd.memset(raw[:].bitcast(I32), 0)
        ident = tile("ident", [P, P], F32)
        make_identity(nc, ident[:])
        ww_raw = [tile("ww_raw%d" % i, [P, 2 * S], U8) for i in range(3)]
        offs_t = load_list("offs_t", offs)
        load_scale_rows(xs_all, x_scales, (nc.sync, nc.sync, nc.scalar, nc.scalar))
        nc.sync.dma_start(ww_raw[0][:].bitcast(I32), w1_words[0].bitcast(I32))
        xw_all = tile("xw_all", [P, T], I32)
        nc.sync.dma_start(xw_all[:], x_words[0].rearrange("p n t -> p (n t)").bitcast(I32))
        load_scale_rows(ws_raw[0], w1_scales, (nc.sync,) * 4)
        n2_t = load_list("n2_t", n2)
        n1_t = load_list("n1_t", n1)
        n4_t = load_list("n4_t", n4)
        n3_t = load_list("n3_t", n3)
        gn_t = tile("gn_t", [P, PACK], F32)
        nc.sync.dma_start(gn_t[:], gn.rearrange("(p t) o -> p (t o)", t=PACK))
        nc.sync.dma_start(ww_raw[1][:].bitcast(I32), w2_words[0].bitcast(I32))
        nc.sync.dma_start(ww_raw[2][:].bitcast(I32), w3_words[0].bitcast(I32))
        load_scale_rows(ws_raw[1], w2_scales, (nc.sync,) * 4)
        load_scale_rows(ws_raw[2], w3_scales, (nc.sync,) * 4)
        gm_t = tile("gm_t", [P, PACK], F32)
        nc.sync.dma_start(gm_t[:], gm.rearrange("(p t) o -> p (t o)", t=PACK))
        n5_t = load_list("n5_t", n5)
        n6_t = load_list("n6_t", n6)

        ww = [tile("ww%d" % i, [P, 2 * S], U8) for i in range(3)]
        ws = [tile("ws%d" % i, [P, S], U8) for i in range(3)]

        def deal(i):
            if i == 0:
                nc.scalar.copy(
                    ww[i][:].bitcast(U16).rearrange("p (t m) -> p t m", t=PACK),
                    ww_raw[i][:].bitcast(U16).rearrange("p (m t) -> p t m", t=PACK),
                )
            else:
                nc.gpsimd.tensor_copy(
                    ww[i][:].rearrange("p (t m b) -> p t m b", t=PACK, b=2),
                    ww_raw[i][:].rearrange("p (m t b) -> p t m b", t=PACK, b=2),
                )
            nc.gpsimd.tensor_copy(
                ws[i][:].rearrange("p (t m) -> p t m", t=PACK),
                ws_raw[i][:].rearrange("p (m t) -> p t m", t=PACK),
            )

        def product(dst, i, t, codes, scales, cols, start, stop):
            nc.tensor.matmul_mx(
                out=dst,
                lhsT=ww[i][:, 2 * P * t : 2 * P * (t + 1)].bitcast(FP4X4),
                lhsT_scale=ws[i][:, P * t : P * (t + 1)],
                rhs=codes[:, cols].bitcast(FP8X4),
                rhs_scale=scales[:, cols],
                start=start,
                stop=stop,
            )

        xs = tile("xs", [P, S], U8)
        xw = tile("xw", [P, S], U32)
        nc.vector.tensor_copy(xs[:], xs_all[:].indirect(offs_t[:]))
        deal(0)
        halves = [slice(0, HALF), slice(HALF, S)]
        for u in range(2):
            nc.vector.tensor_copy(xw[:, halves[u]], xw_all[:].bitcast(U32).indirect(half(offs_t, u)))

        y_bank = [psum.tile([P, S], F32, name="y_bank%d" % t, tag="a%d" % t) for t in range(PACK)]
        y_first = psum.tile([P, HALF], F32, name="y_first", tag="b3")
        product(y_first[:], 0, 0, xw, xs, halves[0], True, True)
        product(y_bank[0][:, halves[1]], 0, 0, xw, xs, halves[1], True, True)
        for t in range(1, PACK):
            for u in range(2):
                product(y_bank[t][:, halves[u]], 0, t, xw, xs, halves[u], True, True)

        gain = tile("gain", [P, PACK], F32)
        nc.gpsimd.tensor_scalar(gain[:], gn_t[:], 0.5, 0.0, ALU.mult, ALU.add)

        def gather(engine, dst, window, offsets):
            if engine is nc.vector:
                nc.vector.tensor_copy(dst, window[:].indirect(offsets))
            else:
                nc.scalar.activation(dst, window[:].indirect(offsets), ACT.Copy)

        def planes(name):
            return [tile("%s%d" % (name, t), [P, S], F32) for t in range(PACK)]

        y, y2, sm, ex, ex3, ex4, th = (planes(n) for n in ("y", "y2", "sm", "ex", "ex3", "ex4", "th"))
        gate = planes("gate")
        ds = [tile("ds%d" % t, [P, 2 * S], F32) for t in range(PACK)]
        den_bank = [psum.tile([P, PACK, P], F32, name="den_bank%d" % j, tag="b%d" % j) for j in range(PACK)]

        def take_y(t):
            if t == 0:
                nc.scalar.copy(y[t][:, halves[0]], y_first[:])
                nc.vector.tensor_copy(y[t][:, halves[1]], y_bank[t][:, halves[1]])
            else:
                nc.scalar.copy(y[t][:], y_bank[t][:])

        def fetch_y(t, engine):
            for u in range(2):
                gather(engine, y2[t][:, halves[u]], y[t], half(n2_t, u))

        def send(t):
            nc.vector.tensor_tensor(sm[t][:], y2[t][:], (y_bank[t] if t else y[t])[:], ALU.max)
            nc.vector.tensor_copy(ds[t][:].indirect(n1_t[:]), sm[t][:])

        def funcs(t, cols=slice(0, S)):
            nc.scalar.activation(ex[t][:, cols], (y_bank[t] if t else y[t])[:, cols], ACT.Exp, scale=0.5)

        def tanh(t):
            nc.scalar.activation(th[t][:], y[t][:], ACT.Tanh, scale=0.5)
            nc.gpsimd.tensor_scalar(gate[t][:], th[t][:], gain[:, t : t + 1], gain[:, t : t + 1], ALU.mult, ALU.add)

        def fetch_ex(t, e3, e4):
            for u in range(2):
                gather(e3, ex3[t][:, halves[u]], ex[t], half(n3_t, u))
            for u in range(2):
                gather(e4, ex4[t][:, halves[u]], ex[t], half(n4_t, u))
            for j in range(PACK):
                for k, src in enumerate((ex[t], ex3[t], ex4[t])):
                    nc.tensor.matmul(
                        den_bank[j][:, t, :], src[:, P * j : P * (j + 1)], ident[:],
                        start=(k == 0), stop=(k == 2), is_transpose=True,
                    )

        V, A = nc.vector, nc.scalar
        deal(1)
        deal(2)
        zp = tile("zp", [P, PACK, S], BF16)
        z2p = tile("z2p", [P, PACK, S], BF16)

        def make_z(t):
            for cols in halves if t == PACK - 1 else [slice(0, S)]:
                nc.gpsimd.tensor_tensor(zp[:, t, cols], gate[t][:, cols], ds[t][:, cols], ALU.mult)

        def quantised(name):
            return (tile(name + "_woven", [P, S * PACK], BF16), tile(name + "_codes", [P, S], U32),
                    tile(name + "_scales", [P, S], U8))

        def weave(copy, dst, src, u):
            copy(
                dst[0][:, PACK * HALF * u : PACK * HALF * (u + 1)].rearrange("p (c i t) -> p c t i", i=4, t=PACK),
                src[:, :, halves[u]].rearrange("p t (c i) -> p c t i", i=4),
            )

        def quantise(dst, u):
            nc.vector.quantize_mx(
                out=dst[1][:, halves[u]].bitcast(FP8X4),
                scales=dst[2][:, halves[u]],
                in_=dst[0][:, PACK * HALF * u : PACK * HALF * (u + 1)],
            )

        take_y(0)
        fetch_y(0, V)
        funcs(0)
        take_y(1)
        fetch_ex(0, A, V)
        send(0)
        funcs(1)
        funcs(2, halves[0])
        fetch_y(1, A)
        funcs(2, halves[1])
        take_y(2)
        fetch_ex(2, A, V)
        send(1)
        tanh(0)
        make_z(0)
        funcs(3, halves[0])
        fetch_y(2, A)
        funcs(3, halves[1])
        take_y(3)
        fetch_ex(3, A, V)
        send(2)
        tanh(1)
        make_z(1)
        fetch_y(3, A)
        fetch_ex(1, A, A)
        send(3)
        tanh(2)
        make_z(2)
        tanh(3)
        make_z(3)
        zq, z2q = quantised("z"), quantised("z2")

        root = tile("root", [P, PACK, S], F32)
        rden = tile("rden", [P, PACK, S], F32)
        r_bank = [psum.tile([P, 2, HALF], F32, name="r_bank%d" % b, tag="a%d" % b) for b in range(PACK)]
        for u in range(2):
            for j, cols in ((2 * u, slice(0, S)), (2 * u + 1, halves[0]), (2 * u + 1, halves[1])):
                den = den_bank[j][:].rearrange("p t n -> p (t n)")
                nc.scalar.activation(root[:, j, cols], den[:, cols], ACT.Abs_reciprocal_sqrt, scale=0.5)
            for t in range(PACK):
                if t % 2 == 0:
                    blocks, cols = slice(2 * u, 2 * u + 2), slice(P * t, P * (t + 2))
                    nc.scalar.activation(rden[:, blocks, cols], root[:, blocks, cols], ACT.Square)
                for jj in range(2):
                    nc.tensor.transpose(
                        r_bank[2 * u + t // 2][:, t % 2, P * jj : P * (jj + 1)],
                        rden[:, 2 * u + jj, P * t : P * (t + 1)], ident[:],
                    )
        for u in range(2):
            weave(nc.scalar.copy, zq, zp, u)
        h_bank = [[None] * PACK, [None] * PACK]
        h = planes("h")
        for u in range(2):
            for t in range(PACK):
                nc.vector.scalar_tensor_tensor(
                    z2p[:, t, halves[u]], ex[t][:, halves[u]], gm_t[:, t : t + 1], r_bank[2 * u + t // 2][:, t % 2, :],
                    ALU.mult, ALU.mult,
                )
            quantise(zq, u)
            weave(nc.vector.tensor_copy, z2q, z2p, u)
            quantise(z2q, u)
            for t in range(PACK):
                h_bank[u][t] = psum.tile([P, HALF], F32, name="h_bank%d%d" % (u, t), tag="ba"[u] + str(t))
            if u == 1:
                product(h_bank[u][0][:], 1, 0, zq[1], zq[2], halves[u], True, False)
                product(h_bank[u][0][:], 2, 0, z2q[1], z2q[2], halves[u], False, True)
            for t in range(u, PACK):
                product(h_bank[u][t][:], 2, t, z2q[1], z2q[2], halves[u], True, False)
            for t in range(u, PACK):
                product(h_bank[u][t][:], 1, t, zq[1], zq[2], halves[u], False, True)
        for t in range(PACK):
            nc.scalar.copy(h[t][:, halves[0]], h_bank[0][t][:])

        res = planes("res")
        npa = tile("npa", [P, PACK, HALF], F32)
        pb = tile("pb", [P, PACK, HALF], F32)
        rb = tile("rb", [P, PACK, HALF], F32)
        out_rows = out_0.rearrange("(p t) n -> p t n", t=PACK)
        o_woven = tile("o_woven", [P, S, PACK], BF16)
        o_codes = tile("o_codes", [P, S], I32)
        o_scales = tile("o_scales", [P, S], U8)
        for t in range(PACK):
            nc.scalar.copy(h[t][:, halves[1]], h_bank[1][t][:])
            nc.scalar.activation(npa[:, t, :], h[t][:].indirect(n5_t[:]), ACT.Copy, scale=-1.0)
            gather(V if t == 0 else A, pb[:, t, :], h[t], n6_t[:])

        def put_a(t):
            nc.vector.tensor_tensor(res[t][:].indirect(n5_t[:]), pb[:, t, :], npa[:, t, :], ALU.add)

        def put_b(t):
            nc.vector.tensor_copy(res[t][:].indirect(n6_t[:]), rb[:, t, :])
            nc.sync.dma_start(out_rows[:, t, :], res[t][:])
            nc.scalar.copy(o_woven[:, halves[0], t], res[t][:, halves[0]])
            if t < 2:
                nc.scalar.copy(o_woven[:, halves[1], t], res[t][:, halves[1]])
            else:
                nc.vector.tensor_copy(o_woven[:, halves[1], t], res[t][:, halves[1]])

        for t in (0, 2):
            put_a(t)
            nc.vector.scalar_tensor_tensor(
                rb[:, t : t + 2, :], npa[:, t : t + 2, :], -0.5, pb[:, t : t + 2, :], ALU.mult, ALU.max
            )
            put_a(t + 1)
            put_b(t)
            put_b(t + 1)
        words_out = out_1[0].rearrange("p n t -> p (n t)").bitcast(I32)
        for u in (1, 0):
            nc.vector.quantize_mx(
                out=o_codes[:, halves[u]].bitcast(FP8X4),
                scales=o_scales[:, halves[u]],
                in_=o_woven[:, halves[u], :].rearrange("p n t -> p (n t)"),
            )
            nc.sync.dma_start(words_out[:, halves[u]], o_codes[:, halves[u]])
        for q in range(4):
            queue = nc.scalar if q % 2 else nc.sync
            queue.dma_start(out_2[0, 4 * q : 4 * q + 4, :].bitcast(I32), o_scales[32 * q : 32 * q + 4, :].bitcast(I32))
